import numpy as np
import ml_dtypes

BF16 = ml_dtypes.bfloat16


def bf(x):
    return np.asarray(x, np.float32).astype(BF16)


def f32(x):
    return np.asarray(x, np.float32)


def f64(x):
    return np.asarray(x).astype(np.float64)


def striped(idx):
    return np.concatenate([l.reshape(-1, 16).T for l in idx])


def rows(idx, k):
    return np.tile(np.repeat(idx, 16, axis=0), (k // (16 * 8), 1))


def look(tab, idx):
    return np.take_along_axis(f64(tab), rows(idx, len(tab)), axis=1)


K, S, V, N, M = 128, 2048, 1536, 1536, 512


def silu(v):
    return v / (1.0 + np.exp(-v))


def setup_inputs():
    return {"tab": f32(np.random.standard_normal((2, K, S))), "w": bf(np.random.standard_normal((K, M)) / np.sqrt(K)), "b": f32(0.5 * np.random.standard_normal((M, 1))), "offs": striped(np.stack([np.random.permutation(S)[:N] for _ in range(8)]))}


def reference(tab, w, b, offs):
    idx = np.stack([g.T.reshape(-1) for g in np.split(offs, 8)])
    x = (np.minimum(np.maximum(look(tab[0], idx), -1.25), 1.0)) * (silu(look(tab[1], idx)))
    return np.maximum(f64(w).T @ x + f64(b), 0.0)

@@ -1,0 +1,67 @@
+import concourse.mybir as mybir
+
+F32, BF16, U16 = mybir.dt.float32, mybir.dt.bfloat16, mybir.dt.uint16
+ALU = mybir.AluOpType
+ACT = mybir.ActivationFunctionType
+
+P = 128
+S = 2048
+N = 1536
+M = 512
+PIECE = 512
+PIECES = N // PIECE
+ROWS = M // P
+FLOPS = 2 * P * M * N
+
+
+def tile_lookup_vg_clipsilu_relu_kernel(tc, tab, w, b, offs, out):
+    nc = tc.nc
+    b_rows = b.rearrange("(p t) one -> p (t one)", t=ROWS)
+    out_rows = out.rearrange("(p t) i -> p t i", t=ROWS)
+    with (
+        tc.tile_pool(name="held", bufs=1) as held,
+        tc.tile_pool(name="ring", bufs=PIECES) as ring,
+        tc.tile_pool(name="results", bufs=PIECES * ROWS) as results,
+        tc.psum_pool(name="psum", bufs=8) as psum,
+    ):
+        offsets = held.tile([P, N // 16], U16, name="offsets")
+        values = held.tile([P, S], F32, name="values")
+        gates = held.tile([P, S], F32, name="gates")
+        weights = held.tile([P, M], BF16, name="weights")
+        bias = held.tile([P, ROWS], F32, name="bias")
+        nc.sync.dma_start(offsets[:], offs)
+        nc.sync.dma_start(values[:], tab[0])
+        nc.sync.dma_start(gates[:], tab[1])
+        nc.sync.dma_start(weights[:], w)
+        nc.sync.dma_start(bias[:], b_rows)
+
+        def entries(piece):
+            return offsets[:, piece * (PIECE // 16) : (piece + 1) * (PIECE // 16)]
+
+        def look_up_values(piece):
+            clamped = ring.tile([P, PIECE], F32, name="clamped")
+            nc.vector.tensor_scalar(clamped[:], values[:].indirect(entries(piece)), -1.25, 1.0, ALU.max, ALU.min)
+            return clamped
+
+        def look_up_gates(piece):
+            gated = ring.tile([P, PIECE], F32, name="gated")
+            nc.scalar.activation(gated[:], gates[:].indirect(entries(piece)), ACT.Silu)
+            return gated
+
+        clamped = [look_up_values(piece) for piece in range(PIECES)]
+        gated = [look_up_gates(0)]
+        for piece in range(PIECES):
+            if piece + 1 < PIECES:
+                gated.append(look_up_gates(piece + 1))
+            x = ring.tile([P, PIECE], BF16, name="x")
+            nc.vector.tensor_tensor(x[:], clamped[piece][:], gated[piece][:], ALU.mult)
+            columns = slice(piece * PIECE, (piece + 1) * PIECE)
+            for t in range(ROWS):
+                product = psum.tile([P, PIECE], F32, name="product")
+                nc.tensor.matmul(product[:], weights[:, t::ROWS], x[:], start=True, stop=True)
+                result = results.tile([P, PIECE], F32, name="result")
+                if t % 2 == 0:
+                    nc.vector.tensor_scalar(result[:], product[:], bias[:, t : t + 1], 0.0, ALU.add, ALU.max)
+                else:
+                    nc.scalar.activation(result[:], product[:], ACT.Relu, bias=bias[:, t : t + 1])
+                nc.sync.dma_start(out_rows[:, t, columns], result[:])

@@ -35,6 +35,11 @@ def tile_lookup_vg_clipsilu_relu_kernel(tc, tab, w, b, offs, out):
         nc.sync.dma_start(weights[:], w)
         nc.sync.dma_start(bias[:], b_rows)
 
+        warm = held.tile([P, 1], F32, name="warm")
+        warmed = held.tile([P, 1], F32, name="warmed")
+        nc.gpsimd.memset(warm[:], 0.0)
+        nc.scalar.activation(warmed[:], warm[:], ACT.Silu)
+
         def entries(piece):
             return offsets[:, piece * (PIECE // 16) : (piece + 1) * (PIECE // 16)]
 

@@ -21,7 +21,7 @@ def tile_lookup_vg_clipsilu_relu_kernel(tc, tab, w, b, offs, out):
     with (
         tc.tile_pool(name="held", bufs=1) as held,
         tc.tile_pool(name="ring", bufs=PIECES) as ring,
-        tc.tile_pool(name="results", bufs=PIECES * ROWS) as results,
+        tc.tile_pool(name="results", bufs=PIECES * ROWS // 2) as results,
         tc.psum_pool(name="psum", bufs=8) as psum,
     ):
         offsets = held.tile([P, N // 16], U16, name="offsets")
@@ -61,12 +61,13 @@ def tile_lookup_vg_clipsilu_relu_kernel(tc, tab, w, b, offs, out):
             x = ring.tile([P, PIECE], BF16, name="x")
             nc.vector.tensor_tensor(x[:], clamped[piece][:], gated[piece][:], ALU.mult)
             columns = slice(piece * PIECE, (piece + 1) * PIECE)
-            for t in range(ROWS):
-                product = psum.tile([P, PIECE], F32, name="product")
-                nc.tensor.matmul(product[:], weights[:, t::ROWS], x[:], start=True, stop=True)
-                result = results.tile([P, PIECE], F32, name="result")
-                if t % 2 == 0:
-                    nc.vector.tensor_scalar(result[:], product[:], bias[:, t : t + 1], 0.0, ALU.add, ALU.max)
-                else:
-                    nc.scalar.activation(result[:], product[:], ACT.Relu, bias=bias[:, t : t + 1])
-                nc.sync.dma_start(out_rows[:, t, columns], result[:])
+            for pair in range(0, ROWS, 2):
+                result = results.tile([P, 2, PIECE], F32, name="result")
+                for t in (pair, pair + 1):
+                    product = psum.tile([P, PIECE], F32, name="product")
+                    nc.tensor.matmul(product[:], weights[:, t::ROWS], x[:], start=True, stop=True)
+                    if t % 2 == 0:
+                        nc.vector.tensor_scalar(result[:, 0, :], product[:], bias[:, t : t + 1], 0.0, ALU.add, ALU.max)
+                    else:
+                        nc.scalar.activation(result[:, 1, :], product[:], ACT.Relu, bias=bias[:, t : t + 1])
+                nc.sync.dma_start(out_rows[:, pair : pair + 2, columns], result[:])

@@ -21,7 +21,7 @@ def tile_lookup_vg_clipsilu_relu_kernel(tc, tab, w, b, offs, out):
     with (
         tc.tile_pool(name="held", bufs=1) as held,
         tc.tile_pool(name="ring", bufs=PIECES) as ring,
-        tc.tile_pool(name="results", bufs=PIECES * ROWS // 2) as results,
+        tc.tile_pool(name="results", bufs=(PIECES + 1) * ROWS) as results,
         tc.psum_pool(name="psum", bufs=8) as psum,
     ):
         offsets = held.tile([P, N // 16], U16, name="offsets")
@@ -58,16 +58,18 @@ def tile_lookup_vg_clipsilu_relu_kernel(tc, tab, w, b, offs, out):
         for piece in range(PIECES):
             if piece + 1 < PIECES:
                 gated.append(look_up_gates(piece + 1))
-            x = ring.tile([P, PIECE], BF16, name="x")
-            nc.vector.tensor_tensor(x[:], clamped[piece][:], gated[piece][:], ALU.mult)
-            columns = slice(piece * PIECE, (piece + 1) * PIECE)
-            for pair in range(0, ROWS, 2):
-                result = results.tile([P, 2, PIECE], F32, name="result")
-                for t in (pair, pair + 1):
-                    product = psum.tile([P, PIECE], F32, name="product")
+            width = PIECE // 2 if piece == 0 else PIECE
+            for start in range(0, PIECE, width):
+                part = slice(start, start + width)
+                x = ring.tile([P, width], BF16, name="x")
+                nc.vector.tensor_tensor(x[:], clamped[piece][:, part], gated[piece][:, part], ALU.mult)
+                columns = slice(piece * PIECE + start, piece * PIECE + start + width)
+                for t in range(ROWS):
+                    product = psum.tile([P, width], F32, name="product")
                     nc.tensor.matmul(product[:], weights[:, t::ROWS], x[:], start=True, stop=True)
+                    result = results.tile([P, width], F32, name="result")
                     if t % 2 == 0:
-                        nc.vector.tensor_scalar(result[:, 0, :], product[:], bias[:, t : t + 1], 0.0, ALU.add, ALU.max)
+                        nc.vector.tensor_scalar(result[:], product[:], bias[:, t : t + 1], 0.0, ALU.add, ALU.max)
                     else:
-                        nc.scalar.activation(result[:, 1, :], product[:], ACT.Relu, bias=bias[:, t : t + 1])
-                nc.sync.dma_start(out_rows[:, pair : pair + 2, columns], result[:])
+                        nc.scalar.activation(result[:], product[:], ACT.Relu, bias=bias[:, t : t + 1])
+                    nc.sync.dma_start(out_rows[:, t, columns], result[:])

import concourse.mybir as mybir

F32, BF16, U16 = mybir.dt.float32, mybir.dt.bfloat16, mybir.dt.uint16
ALU = mybir.AluOpType
ACT = mybir.ActivationFunctionType

P = 128
S = 2048
N = 1536
M = 512
PIECE = 512
PIECES = N // PIECE
ROWS = M // P
FLOPS = 2 * P * M * N


def tile_lookup_vg_clipsilu_relu_kernel(tc, tab, w, b, offs, out):
    nc = tc.nc
    b_rows = b.rearrange("(p t) one -> p (t one)", t=ROWS)
    out_rows = out.rearrange("(p t) i -> p t i", t=ROWS)
    with (
        tc.tile_pool(name="held", bufs=1) as held,
        tc.tile_pool(name="ring", bufs=PIECES) as ring,
        tc.tile_pool(name="results", bufs=(PIECES + 1) * ROWS) as results,
        tc.psum_pool(name="psum", bufs=8) as psum,
    ):
        offsets = held.tile([P, N // 16], U16, name="offsets")
        values = held.tile([P, S], F32, name="values")
        gates = held.tile([P, S], F32, name="gates")
        weights = held.tile([P, M], BF16, name="weights")
        bias = held.tile([P, ROWS], F32, name="bias")
        nc.sync.dma_start(offsets[:], offs)
        nc.sync.dma_start(values[:], tab[0])
        nc.sync.dma_start(gates[:], tab[1])
        nc.sync.dma_start(weights[:], w)
        nc.sync.dma_start(bias[:], b_rows)

        warm = held.tile([P, 1], F32, name="warm")
        warmed = held.tile([P, 1], F32, name="warmed")
        nc.gpsimd.memset(warm[:], 0.0)
        nc.scalar.activation(warmed[:], warm[:], ACT.Silu)

        def entries(piece):
            return offsets[:, piece * (PIECE // 16) : (piece + 1) * (PIECE // 16)]

        def look_up_values(piece):
            clamped = ring.tile([P, PIECE], F32, name="clamped")
            nc.vector.tensor_scalar(clamped[:], values[:].indirect(entries(piece)), -1.25, 1.0, ALU.max, ALU.min)
            return clamped

        def look_up_gates(piece):
            gated = ring.tile([P, PIECE], F32, name="gated")
            nc.scalar.activation(gated[:], gates[:].indirect(entries(piece)), ACT.Silu)
            return gated

        clamped = [look_up_values(piece) for piece in range(PIECES)]
        gated = [look_up_gates(0)]
        for piece in range(PIECES):
            if piece + 1 < PIECES:
                gated.append(look_up_gates(piece + 1))
            width = PIECE // 2 if piece == 0 else PIECE
            for start in range(0, PIECE, width):
                part = slice(start, start + width)
                x = ring.tile([P, width], BF16, name="x")
                nc.vector.tensor_tensor(x[:], clamped[piece][:, part], gated[piece][:, part], ALU.mult)
                columns = slice(piece * PIECE + start, piece * PIECE + start + width)
                for t in range(ROWS):
                    product = psum.tile([P, width], F32, name="product")
                    nc.tensor.matmul(product[:], weights[:, t::ROWS], x[:], start=True, stop=True)
                    result = results.tile([P, width], F32, name="result")
                    if t % 2 == 0:
                        nc.vector.tensor_scalar(result[:], product[:], bias[:, t : t + 1], 0.0, ALU.add, ALU.max)
                    else:
                        nc.scalar.activation(result[:], product[:], ACT.Relu, bias=bias[:, t : t + 1])
                    nc.sync.dma_start(out_rows[:, t, columns], result[:])
